import numpy as np
import ml_dtypes


def mxq(x, axis, fmt="e4m3"):
    dtype, down = {"e4m3": (ml_dtypes.float8_e4m3fn, 7), "e5m2": (ml_dtypes.float8_e5m2, 14)}[fmt]
    v = np.moveaxis(np.asarray(x, np.float32).astype(ml_dtypes.bfloat16).astype(np.float64), axis, -1)
    blocks = v.reshape(v.shape[:-1] + (-1, 32))
    amax = np.abs(blocks).max(-1, keepdims=True)
    byte = np.maximum(np.where(amax > 0, np.frexp(amax)[1] - 1 + 127, 0) - down, 1)
    scale = np.exp2(byte - 127.0)
    codes = (blocks / scale).astype(np.float32).astype(dtype).astype(np.float64)
    return np.moveaxis((codes * scale).reshape(v.shape), -1, axis)


WIDE = False


def mx_kscale(k):
    if not WIDE:
        return np.ones(k)
    levels = np.array([10, -10, 5, -5, 0])
    if k % 512:
        return np.exp2(np.random.permutation(np.resize(levels, k // 32))).repeat(32)
    a = np.empty((k // 512, 16))
    for p in range(k // 512):
        a[p, :8] = np.random.permutation(np.resize(levels, 8))
        for g in range(8):
            far = levels[np.abs(levels - a[p, g]) >= 10]
            a[p, g + 8] = far[np.random.randint(len(far))]
    return np.exp2(a.ravel()).repeat(32)


def f64(x):
    return np.asarray(x).astype(np.float64)


def striped(idx):
    return np.tile(np.asarray(idx).reshape(-1, 16).T, (8, 1)).astype(np.uint16)


def unstriped(offs):
    return offs[:16].T.reshape(-1).astype(np.int64)


E2M1 = np.array([0.0, 0.5, 1.0, 1.5, 2.0, 3.0, 4.0, 6.0, -0.0, -0.5, -1.0, -1.5, -2.0, -3.0, -4.0, -6.0])


def pack_weight(w, fmt):
    k, n = w.shape
    w = f64(np.asarray(w, np.float32).astype(ml_dtypes.bfloat16)).reshape(k // 32, 32, n)
    amax = np.abs(w).max(1)
    if fmt == "e4m3":
        byte = np.frexp(amax)[1] - 1 + 127 - 7
    else:
        mant, ex = np.frexp(amax / 6.0)
        byte = np.where(mant > 0.5, ex, ex - 1) + 127
    byte = np.clip(np.where(amax > 0, byte, 1), 1, 254)
    scaled = (w * np.exp2(127.0 - byte)[:, None, :]).reshape(k, n).astype(np.float32)
    by_word = np.ascontiguousarray(scaled.reshape(k // 512, 128, 4, n).transpose(0, 1, 3, 2))
    if fmt == "e4m3":
        words = by_word.astype(ml_dtypes.float8_e4m3fn).view(np.uint8)
    else:
        c = by_word.astype(ml_dtypes.float4_e2m1fn).view(np.uint8) & 0xF
        words = (c[..., 0::2] | (c[..., 1::2] << 4)).reshape(k // 512, 128, 2 * n)
    return np.ascontiguousarray(words), np.ascontiguousarray(byte.astype(np.uint8).reshape(k // 512, 16, n))


def unpack_weight(words, scales, fmt):
    g, _, n = scales.shape
    words = np.ascontiguousarray(words).reshape(g, 128, n, -1)
    if fmt == "e4m3":
        vals = words.view(ml_dtypes.float8_e4m3fn).astype(np.float64)
    else:
        nib = np.empty((g, 128, n, 4), np.uint8)
        nib[..., 0::2] = words & 0xF
        nib[..., 1::2] = words >> 4
        vals = E2M1[nib]
    vals = vals * np.repeat(np.exp2(scales.astype(np.float64) - 127.0), 8, axis=1)[..., None]
    return vals.transpose(0, 1, 3, 2).reshape(g * 512, n)


def bf(x):
    return np.asarray(x, np.float32).astype(ml_dtypes.bfloat16)


def planes(Y):
    r, m = Y.shape
    b = f64(bf(Y)).reshape(r // 32, 32, m)
    amax = np.abs(b).max(1)
    byte = np.clip(np.where(amax > 0, np.frexp(amax)[1] - 1 + 127 - 7, 1), 1, 254)
    codes = (b * np.exp2(127.0 - byte)[:, None, :]).reshape(r, m).astype(np.float32).astype(ml_dtypes.float8_e4m3fn).view(np.uint8)
    words = codes.reshape(r // 512, 128, 4, m).transpose(0, 1, 3, 2)
    return np.ascontiguousarray(words), np.ascontiguousarray(byte.astype(np.uint8).reshape(r // 512, 16, m))


K, T, J, R, N = 1024, 1024, 512, 512, 512


def setup_inputs():
    n = np.random.standard_normal
    idx = np.random.permutation(T)[:J]
    fk = mx_kscale(K)
    fr = mx_kscale(R)
    wap = pack_weight(n((K, R)) * 1 / np.sqrt(K) * fk[:, None], "e4m3")
    wbp = pack_weight(n((R, N)) * 1 / np.sqrt(R) / fr[:, None], "e2m1")
    return {
        "xt": (n((K, T)) * np.random.uniform(0.3, 1.9, (1, T)) / fk[:, None]).astype(np.float32),
        "wa_words": wap[0],
        "wa_scales": wap[1],
        "fr": (np.random.uniform(0.5, 2.0, (R, 1)) * fr[:, None]).astype(np.float32),
        "wb_words": wbp[0],
        "wb_scales": wbp[1],
        "res": (1.0 * n((N, T))).astype(np.float32),
        "offs": striped(idx),
    }


def reference(xt, wa_words, wa_scales, fr, wb_words, wb_scales, res, offs):
    idx = unstriped(offs)
    wau = unpack_weight(wa_words, wa_scales, "e4m3")
    wbu = unpack_weight(wb_words, wb_scales, "e2m1")
    xtidxq = mxq(f64(xt)[:, idx], 0, "e4m3")
    z = xtidxq.T @ wau
    d = z - np.mean(z, axis=1, keepdims=True)
    e = d / np.sqrt(np.mean(np.square(d), axis=1, keepdims=True) + 0.01)
    et = e.T
    hid = et * f64(fr)
    hidq = mxq(hid, 0, "e4m3")
    p = wbu.T @ hidq
    pp = np.zeros((N, T))
    pp[:, idx] = p
    y = pp + 0.3 * f64(res)
    words, scales = planes(y)
    return y, words, scales

@@ -1,0 +1,289 @@
+from contextlib import ExitStack
+
+import concourse.mybir as mybir
+from concourse.masks import make_identity
+
+K, T, J, R, N = 1024, 1024, 512, 512, 512
+FLOPS = 2 * J * K * R + 2 * J * R * N
+
+F32 = mybir.dt.float32
+BF16 = mybir.dt.bfloat16
+I32 = mybir.dt.int32
+U32 = mybir.dt.uint32
+U16 = mybir.dt.uint16
+U8 = mybir.dt.uint8
+FP8X4 = mybir.dt.float8_e4m3fn_x4
+FP4X4 = mybir.dt.float4_e2m1fn_x4
+ALU = mybir.AluOpType
+ACT = mybir.ActivationFunctionType
+
+P = 128
+PACK = 4
+CH = 128
+NCH = J // CH
+OC = CH // 16
+EPS = 0.01
+RES_GAIN = 0.3
+QT = 256
+
+
+def tile_moe_expert_hidden_rows_levelled_pl_kernel(
+    tc, xt, wa_words, wa_scales, fr, wb_words, wb_scales, res, offs, out_0, out_1, out_2
+):
+    nc = tc.nc
+    with ExitStack() as ctx:
+        keep = ctx.enter_context(tc.tile_pool(name="keep", bufs=1))
+        psum = ctx.enter_context(tc.psum_pool(name="psum", bufs=1))
+
+        def sb(name, width, dtype):
+            return keep.tile([P, width], dtype, name=name, align_bytes=64)
+
+        offsets = keep.tile([P, J // 16], U16, name="offsets")
+        nc.sync.dma_start(offsets[:], offs)
+
+        wa_plane = sb("wa_plane", 2 * R, U8)
+        wb_plane_raw = sb("wb_plane_raw", N, U8)
+        nc.vector.memset(wa_plane[:].bitcast(I32), 0)
+        nc.vector.memset(wb_plane_raw[:].bitcast(I32), 0)
+        warm = sb("warm", 2, F32)
+        nc.vector.memset(warm[:, 0:1], 1.0)
+        nc.scalar.activation(warm[:, 1:2], warm[:, 0:1], ACT.Abs_reciprocal_sqrt)
+
+        x_rows = xt.rearrange("(z p t) c -> z t p c", p=P, t=PACK)
+        x_sb = [sb(f"x{i}", T, F32) for i in range(2 * PACK)]
+        wa_sb = [sb(f"wa{z}", R, U32) for z in range(2)]
+        wb_raw = sb("wb_raw", 2 * N, U8)
+        fr_sb = sb("fr_sb", PACK, F32)
+        res_sb = [sb(f"res{t}", T, F32) for t in range(PACK)]
+
+        def load_x(i):
+            nc.sync.dma_start(x_sb[i][:], x_rows[i // PACK, i % PACK])
+
+        def load_wa(z):
+            nc.sync.dma_start(wa_sb[z][:].bitcast(I32), wa_words[z].rearrange("p n t -> p (n t)").bitcast(I32))
+
+        def load_wa_scale(r):
+            nc.sync.dma_start(
+                wa_plane[r:P:32, :].bitcast(I32).rearrange("q (z c) -> q z c", z=2),
+                wa_scales.bitcast(I32).rearrange("z (q r) c -> r q z c", r=4)[r],
+            )
+
+        def load_wb_scale(r):
+            nc.scalar.dma_start(
+                wb_plane_raw[r:P:32, :].bitcast(I32),
+                wb_scales[0].bitcast(I32).rearrange("(q r) c -> r q c", r=4)[r],
+            )
+
+        load_x(0)
+        nc.sync.dma_start(wb_raw[:].bitcast(I32), wb_words[0].bitcast(I32))
+        for r in range(4):
+            load_wb_scale(r)
+        load_x(1)
+        load_x(2)
+        load_wa_scale(0)
+        load_wa_scale(1)
+        load_x(3)
+        load_wa_scale(2)
+        load_wa_scale(3)
+        load_x(4)
+        load_x(5)
+        load_x(6)
+        load_wa(0)
+        load_x(7)
+        load_wa(1)
+        nc.sync.dma_start(fr_sb[:], fr.rearrange("(p t) o -> p (t o)", t=PACK))
+        res_rows = res.rearrange("(p t) c -> t p c", t=PACK)
+        for t in range(PACK):
+            nc.sync.dma_start(res_sb[t][:], res_rows[t])
+
+        ident = sb("ident", P, F32)
+        make_identity(nc, ident[:])
+        win = [sb(f"win{t}", T, F32) for t in range(PACK)]
+        for t in range(PACK):
+            (nc.vector if t < 2 else nc.gpsimd).memset(win[t][:], 0.0)
+
+        gath = [sb(f"gath{z}", PACK * J, BF16) for z in range(2)]
+        woven = [sb(f"woven{z}", PACK * J, BF16) for z in range(2)]
+        x_codes = [sb(f"x_codes{z}", J, U32) for z in range(2)]
+        x_plane = [sb(f"x_plane{z}", J, U8) for z in range(2)]
+        z_ps = [psum.tile([P, R], F32, name=f"z{c}") for c in range(NCH)]
+
+        def gath_plane(z, t):
+            return gath[z][:].rearrange("p (c t j) -> p c t j", c=NCH, t=PACK)[:, :, t, :]
+
+        def weave(copy, z, c0, c1):
+            cols = slice(c0 * PACK * CH, c1 * PACK * CH)
+            copy(
+                woven[z][:, cols].rearrange("p (c j t) -> p c j t", j=CH, t=PACK),
+                gath[z][:, cols].rearrange("p (c t j) -> p c j t", j=CH, t=PACK),
+            )
+
+        def quant_x(z, c0, c1):
+            nc.vector.quantize_mx(
+                out=x_codes[z][:, c0 * CH : c1 * CH].bitcast(FP8X4),
+                scales=x_plane[z][:, c0 * CH : c1 * CH],
+                in_=woven[z][:, c0 * PACK * CH : c1 * PACK * CH],
+            )
+
+        def mm1(z, c):
+            cols = slice(c * CH, (c + 1) * CH)
+            nc.tensor.matmul_mx(
+                out=z_ps[c][:],
+                lhsT=x_codes[z][:, cols].bitcast(FP8X4),
+                lhsT_scale=x_plane[z][:, cols],
+                rhs=wa_sb[z][:].bitcast(FP8X4),
+                rhs_scale=wa_plane[:, z * R : (z + 1) * R],
+                start=(z == 0),
+                stop=(z == 1),
+            )
+
+        wb_sb = sb("wb_sb", 2 * N, U8)
+        wb_plane = sb("wb_plane", N, U8)
+        nc.vector.tensor_copy(
+            wb_sb[:].bitcast(U16).rearrange("p (t m) -> p t m", t=PACK),
+            wb_raw[:].bitcast(U16).rearrange("p (m t) -> p t m", t=PACK),
+        )
+        nc.vector.tensor_copy(
+            wb_plane[:].rearrange("p (t m) -> p t m", t=PACK),
+            wb_plane_raw[:].rearrange("p (m t) -> p t m", t=PACK),
+        )
+
+        x_bf = sb("x_bf", T, BF16)
+        nc.scalar.activation(x_bf[:], x_sb[0][:], ACT.Copy)
+        nc.scalar.activation(gath_plane(0, 0), x_bf[:].indirect(offsets[:]), ACT.Copy)
+        for t in range(1, PACK):
+            nc.vector.tensor_copy(gath_plane(0, t), x_sb[t][:].indirect(offsets[:]))
+        for h in range(2):
+            weave(nc.scalar.copy, 0, 2 * h, 2 * h + 2)
+            quant_x(0, 2 * h, 2 * h + 2)
+            mm1(0, 2 * h)
+            mm1(0, 2 * h + 1)
+
+        for t in range(PACK - 1):
+            nc.vector.tensor_copy(gath_plane(1, t), x_sb[PACK + t][:].indirect(offsets[:]))
+        for c in range(NCH):
+            lo = (c * PACK + PACK - 1) * CH
+            nc.vector.tensor_copy(
+                gath[1][:, lo : lo + CH], x_sb[2 * PACK - 1][:].indirect(offsets[:, c * OC : (c + 1) * OC])
+            )
+        for c in range(NCH):
+            weave(nc.scalar.copy, 1, c, c + 1)
+            quant_x(1, c, c + 1)
+            mm1(1, c)
+
+        et_ps = [psum.tile([P, PACK * CH], F32, name=f"et{c}") for c in range(NCH)]
+        for c in range(NCH):
+            stats = sb(f"stats{c}", 6, F32)
+            mv = sb(f"mv{c}", 2, F32)
+            negmean = sb(f"negmean{c}", 1, F32)
+            rstd = sb(f"rstd{c}", 1, F32)
+            shift = sb(f"shift{c}", 1, F32)
+            nc.vector.bn_stats(stats[:], z_ps[c][:])
+            nc.vector.bn_aggr(mv[:], stats[:])
+            nc.scalar.activation(negmean[:], mv[:, 0:1], ACT.Copy, scale=-1.0)
+            nc.scalar.activation(rstd[:], mv[:, 1:2], ACT.Abs_reciprocal_sqrt, bias=EPS)
+            nc.scalar.activation(shift[:], negmean[:], ACT.Copy, scale=rstd[:])
+            e_sb = sb(f"e{c}", R, F32)
+            nc.scalar.activation(
+                e_sb[:].rearrange("p (t m) -> p t m", t=PACK),
+                z_ps[c][:].rearrange("p (m t) -> p t m", t=PACK),
+                ACT.Identity,
+                bias=shift[:],
+                scale=rstd[:],
+            )
+            for t in range(PACK):
+                nc.tensor.transpose(et_ps[c][:, t * CH : (t + 1) * CH], e_sb[:, t * P : (t + 1) * P], ident[:])
+
+        HJ = J // 2
+        p_sb = [[sb(f"p_sb{h}", 2 * HJ, F32)] for h in range(2)]
+        p_late = sb("p_late", 2 * J, F32)
+        for h in range(2):
+            hid = sb(f"hid{h}", PACK * HJ, BF16)
+            for i in range(2):
+                nc.vector.tensor_tensor(
+                    hid[:, i * PACK * CH : (i + 1) * PACK * CH].rearrange("p (j t) -> p j t", t=PACK),
+                    et_ps[2 * h + i][:].rearrange("p (t j) -> p j t", t=PACK),
+                    fr_sb[:].unsqueeze(1).to_broadcast([P, CH, PACK]),
+                    ALU.mult,
+                )
+            h_codes = sb(f"h_codes{h}", HJ, U32)
+            h_plane = sb(f"h_plane{h}", HJ, U8)
+            nc.vector.quantize_mx(out=h_codes[:].bitcast(FP8X4), scales=h_plane[:], in_=hid[:])
+            for u in range(2):
+                p_ps = psum.tile([P, 2 * HJ], F32, name=f"z{2 * h + u}")
+                for i in range(2):
+                    t = 2 * u + i
+                    nc.tensor.matmul_mx(
+                        out=p_ps[:, i * HJ : (i + 1) * HJ],
+                        lhsT=wb_sb[:, 2 * t * P : 2 * (t + 1) * P].bitcast(FP4X4),
+                        lhsT_scale=wb_plane[:, t * P : (t + 1) * P],
+                        rhs=h_codes[:].bitcast(FP8X4),
+                        rhs_scale=h_plane[:],
+                        start=True,
+                        stop=True,
+                    )
+                if u == 0:
+                    nc.scalar.copy(p_sb[h][0][:], p_ps[:])
+                else:
+                    nc.scalar.copy(
+                        p_late[:].rearrange("p (i j) -> p i j", i=2)[:, :, h * HJ : (h + 1) * HJ],
+                        p_ps[:].rearrange("p (i j) -> p i j", i=2),
+                    )
+
+        y_sb = [sb(f"y{h}", 2 * T, F32) for h in range(2)]
+        y_bf = sb("y_bf", PACK * T, BF16)
+        y_codes = sb("y_codes", T, U32)
+        y_plane = sb("y_plane", T, U8)
+        out_rows = out_0.rearrange("(p t) c -> t p c", t=PACK)
+
+        def add(t, c0, c1):
+            lo = (t % 2) * T
+            nc.vector.scalar_tensor_tensor(
+                y_sb[t // 2][:, lo + c0 : lo + c1], res_sb[t][:, c0:c1], RES_GAIN, win[t][:, c0:c1], ALU.mult, ALU.add
+            )
+
+        def store(t, c0, c1):
+            lo = (t % 2) * T
+            nc.sync.dma_start(out_rows[t][:, c0:c1], y_sb[t // 2][:, lo + c0 : lo + c1])
+
+        def pair_views(h, c0, c1):
+            return (
+                y_bf[:, PACK * c0 : PACK * c1].rearrange("p (c h e) -> p c h e", h=2, e=2)[:, :, h, :],
+                y_sb[h][:].rearrange("p (e c) -> p c e", e=2)[:, c0:c1, :],
+            )
+
+        HO = HJ // 16
+        for t in range(2):
+            nc.vector.tensor_copy(win[t][:].indirect(offsets[:, 0:HO]), p_sb[0][0][:, t * HJ : (t + 1) * HJ])
+        for t in range(PACK):
+            if t < 2:
+                nc.vector.tensor_copy(win[t][:].indirect(offsets[:, HO:]), p_sb[1][0][:, t * HJ : (t + 1) * HJ])
+            else:
+                nc.vector.tensor_copy(win[t][:].indirect(offsets[:]), p_late[:, (t - 2) * J : (t - 1) * J])
+            if t < PACK - 1:
+                add(t, 0, T)
+                store(t, 0, T)
+            if t == 1:
+                nc.scalar.copy(*pair_views(0, 0, T))
+        last = PACK - 1
+        for q in range(T // QT):
+            add(last, q * QT, (q + 1) * QT)
+            if q % 2 == 1:
+                store(last, (q - 1) * QT, (q + 1) * QT)
+            if q < 2:
+                nc.scalar.copy(*pair_views(1, q * QT, (q + 1) * QT))
+        for q in range(2, T // QT):
+            nc.vector.tensor_copy(*pair_views(1, q * QT, (q + 1) * QT))
+        words_out = out_1[0].rearrange("p c r -> p (c r)").bitcast(I32)
+        for h in range(2):
+            cols = slice(h * 2 * QT, (h + 1) * 2 * QT)
+            nc.vector.quantize_mx(
+                out=y_codes[:, cols].bitcast(FP8X4),
+                scales=y_plane[:, cols],
+                in_=y_bf[:, h * 2 * QT * PACK : (h + 1) * 2 * QT * PACK],
+            )
+            nc.sync.dma_start(words_out[:, cols], y_codes[:, cols].bitcast(I32))
+        scale_out = out_2[0].bitcast(I32).rearrange("(q r) c -> r q c", r=4)
+        for r in range(4):
+            queue = nc.sync if r % 2 == 0 else nc.scalar
+            queue.dma_start(scale_out[r], y_plane[r:P:32, :].bitcast(I32))

@@ -43,8 +43,8 @@ def tile_moe_expert_hidden_rows_levelled_pl_kernel(
 
         wa_plane = sb("wa_plane", 2 * R, U8)
         wb_plane_raw = sb("wb_plane_raw", N, U8)
-        nc.vector.memset(wa_plane[:].bitcast(I32), 0)
-        nc.vector.memset(wb_plane_raw[:].bitcast(I32), 0)
+        nc.gpsimd.memset(wb_plane_raw[:].bitcast(I32), 0)
+        nc.gpsimd.memset(wa_plane[:].bitcast(I32), 0)
         warm = sb("warm", 2, F32)
         nc.vector.memset(warm[:, 0:1], 1.0)
         nc.scalar.activation(warm[:, 1:2], warm[:, 0:1], ACT.Abs_reciprocal_sqrt)
@@ -69,7 +69,7 @@ def tile_moe_expert_hidden_rows_levelled_pl_kernel(
             )
 
         def load_wb_scale(r):
-            nc.scalar.dma_start(
+            nc.sync.dma_start(
                 wb_plane_raw[r:P:32, :].bitcast(I32),
                 wb_scales[0].bitcast(I32).rearrange("(q r) c -> r q c", r=4)[r],
             )
@@ -78,16 +78,13 @@ def tile_moe_expert_hidden_rows_levelled_pl_kernel(
         nc.sync.dma_start(wb_raw[:].bitcast(I32), wb_words[0].bitcast(I32))
         for r in range(4):
             load_wb_scale(r)
-        load_x(1)
-        load_x(2)
+        for i in range(1, 6):
+            load_x(i)
         load_wa_scale(0)
         load_wa_scale(1)
-        load_x(3)
+        load_x(6)
         load_wa_scale(2)
         load_wa_scale(3)
-        load_x(4)
-        load_x(5)
-        load_x(6)
         load_wa(0)
         load_x(7)
         load_wa(1)
@@ -100,7 +97,7 @@ def tile_moe_expert_hidden_rows_levelled_pl_kernel(
         make_identity(nc, ident[:])
         win = [sb(f"win{t}", T, F32) for t in range(PACK)]
         for t in range(PACK):
-            (nc.vector if t < 2 else nc.gpsimd).memset(win[t][:], 0.0)
+            (nc.vector if t < 1 else nc.gpsimd).memset(win[t][:], 0.0)
 
         gath = [sb(f"gath{z}", PACK * J, BF16) for z in range(2)]
         woven = [sb(f"woven{z}", PACK * J, BF16) for z in range(2)]
@@ -148,87 +145,120 @@ def tile_moe_expert_hidden_rows_levelled_pl_kernel(
             wb_plane_raw[:].rearrange("p (m t) -> p t m", t=PACK),
         )
 
-        x_bf = sb("x_bf", T, BF16)
-        nc.scalar.activation(x_bf[:], x_sb[0][:], ACT.Copy)
-        nc.scalar.activation(gath_plane(0, 0), x_bf[:].indirect(offsets[:]), ACT.Copy)
-        for t in range(1, PACK):
-            nc.vector.tensor_copy(gath_plane(0, t), x_sb[t][:].indirect(offsets[:]))
+        for t in range(PACK):
+            if t in (0, PACK - 1):
+                x_bf = sb(f"x_bf{t}", T, BF16)
+                nc.scalar.activation(x_bf[:], x_sb[t][:], ACT.Copy)
+                nc.scalar.activation(gath_plane(0, t), x_bf[:].indirect(offsets[:]), ACT.Copy)
+            else:
+                nc.vector.tensor_copy(gath_plane(0, t), x_sb[t][:].indirect(offsets[:]))
         for h in range(2):
             weave(nc.scalar.copy, 0, 2 * h, 2 * h + 2)
             quant_x(0, 2 * h, 2 * h + 2)
             mm1(0, 2 * h)
             mm1(0, 2 * h + 1)
 
-        for t in range(PACK - 1):
-            nc.vector.tensor_copy(gath_plane(1, t), x_sb[PACK + t][:].indirect(offsets[:]))
-        for c in range(NCH):
-            lo = (c * PACK + PACK - 1) * CH
+        def gather_first(t):
             nc.vector.tensor_copy(
-                gath[1][:, lo : lo + CH], x_sb[2 * PACK - 1][:].indirect(offsets[:, c * OC : (c + 1) * OC])
+                woven[1][:, 0 : PACK * CH].rearrange("p (j t) -> p t j", t=PACK)[:, t, :],
+                x_sb[PACK + t][:].indirect(offsets[:, 0:OC]),
             )
-        for c in range(NCH):
+
+        def gather_rest(t, c0, c1):
+            nc.vector.tensor_copy(gath_plane(1, t)[:, c0:c1, :], x_sb[PACK + t][:].indirect(offsets[:, c0 * OC : c1 * OC]))
+
+        for t in range(PACK - 1):
+            gather_first(t)
+            gather_rest(t, 1, NCH)
+        gather_first(PACK - 1)
+        gather_rest(PACK - 1, 1, 2)
+        quant_x(1, 0, 1)
+        mm1(1, 0)
+        gather_rest(PACK - 1, 2, NCH)
+        for c in range(1, NCH):
             weave(nc.scalar.copy, 1, c, c + 1)
             quant_x(1, c, c + 1)
             mm1(1, c)
 
         et_ps = [psum.tile([P, PACK * CH], F32, name=f"et{c}") for c in range(NCH)]
-        for c in range(NCH):
+
+        def level(c):
             stats = sb(f"stats{c}", 6, F32)
             mv = sb(f"mv{c}", 2, F32)
-            negmean = sb(f"negmean{c}", 1, F32)
             rstd = sb(f"rstd{c}", 1, F32)
-            shift = sb(f"shift{c}", 1, F32)
+            e_sb = sb(f"e{c}", R, F32)
+            e_view = e_sb[:].rearrange("p (t m) -> p t m", t=PACK)
+            z_view = z_ps[c][:].rearrange("p (m t) -> p t m", t=PACK)
             nc.vector.bn_stats(stats[:], z_ps[c][:])
             nc.vector.bn_aggr(mv[:], stats[:])
-            nc.scalar.activation(negmean[:], mv[:, 0:1], ACT.Copy, scale=-1.0)
             nc.scalar.activation(rstd[:], mv[:, 1:2], ACT.Abs_reciprocal_sqrt, bias=EPS)
-            nc.scalar.activation(shift[:], negmean[:], ACT.Copy, scale=rstd[:])
-            e_sb = sb(f"e{c}", R, F32)
-            nc.scalar.activation(
-                e_sb[:].rearrange("p (t m) -> p t m", t=PACK),
-                z_ps[c][:].rearrange("p (m t) -> p t m", t=PACK),
-                ACT.Identity,
-                bias=shift[:],
-                scale=rstd[:],
-            )
+            if c == 0:
+                nc.vector.tensor_scalar(e_view, z_view, mv[:, 0:1], rstd[:], ALU.subtract, ALU.mult)
+            else:
+                negmean = sb(f"negmean{c}", 1, F32)
+                shift = sb(f"shift{c}", 1, F32)
+                nc.scalar.activation(negmean[:], mv[:, 0:1], ACT.Copy, scale=-1.0)
+                nc.scalar.activation(shift[:], negmean[:], ACT.Copy, scale=rstd[:])
+                nc.scalar.activation(e_view, z_view, ACT.Identity, bias=shift[:], scale=rstd[:])
             for t in range(PACK):
                 nc.tensor.transpose(et_ps[c][:, t * CH : (t + 1) * CH], e_sb[:, t * P : (t + 1) * P], ident[:])
 
-        HJ = J // 2
-        p_sb = [[sb(f"p_sb{h}", 2 * HJ, F32)] for h in range(2)]
-        p_late = sb("p_late", 2 * J, F32)
-        for h in range(2):
-            hid = sb(f"hid{h}", PACK * HJ, BF16)
-            for i in range(2):
+        def hidden_codes(c0, c1):
+            width = (c1 - c0) * CH
+            hid = sb(f"hid{c0}", PACK * width, BF16)
+            for c in range(c0, c1):
+                lo = (c - c0) * PACK * CH
                 nc.vector.tensor_tensor(
-                    hid[:, i * PACK * CH : (i + 1) * PACK * CH].rearrange("p (j t) -> p j t", t=PACK),
-                    et_ps[2 * h + i][:].rearrange("p (t j) -> p j t", t=PACK),
+                    hid[:, lo : lo + PACK * CH].rearrange("p (j t) -> p j t", t=PACK),
+                    et_ps[c][:].rearrange("p (t j) -> p j t", t=PACK),
                     fr_sb[:].unsqueeze(1).to_broadcast([P, CH, PACK]),
                     ALU.mult,
                 )
-            h_codes = sb(f"h_codes{h}", HJ, U32)
-            h_plane = sb(f"h_plane{h}", HJ, U8)
+            h_codes = sb(f"h_codes{c0}", width, U32)
+            h_plane = sb(f"h_plane{c0}", width, U8)
             nc.vector.quantize_mx(out=h_codes[:].bitcast(FP8X4), scales=h_plane[:], in_=hid[:])
-            for u in range(2):
-                p_ps = psum.tile([P, 2 * HJ], F32, name=f"z{2 * h + u}")
-                for i in range(2):
-                    t = 2 * u + i
-                    nc.tensor.matmul_mx(
-                        out=p_ps[:, i * HJ : (i + 1) * HJ],
-                        lhsT=wb_sb[:, 2 * t * P : 2 * (t + 1) * P].bitcast(FP4X4),
-                        lhsT_scale=wb_plane[:, t * P : (t + 1) * P],
-                        rhs=h_codes[:].bitcast(FP8X4),
-                        rhs_scale=h_plane[:],
-                        start=True,
-                        stop=True,
-                    )
-                if u == 0:
-                    nc.scalar.copy(p_sb[h][0][:], p_ps[:])
-                else:
-                    nc.scalar.copy(
-                        p_late[:].rearrange("p (i j) -> p i j", i=2)[:, :, h * HJ : (h + 1) * HJ],
-                        p_ps[:].rearrange("p (i j) -> p i j", i=2),
-                    )
+            return h_codes, h_plane
+
+        def second_layer(operand, planes, bank, dst):
+            h_codes, h_plane = operand
+            width = h_plane.shape[1]
+            p_ps = psum.tile([P, len(planes) * width], F32, name=bank)
+            for i, t in enumerate(planes):
+                nc.tensor.matmul_mx(
+                    out=p_ps[:, i * width : (i + 1) * width],
+                    lhsT=wb_sb[:, 2 * t * P : 2 * (t + 1) * P].bitcast(FP4X4),
+                    lhsT_scale=wb_plane[:, t * P : (t + 1) * P],
+                    rhs=h_codes[:].bitcast(FP8X4),
+                    rhs_scale=h_plane[:],
+                    start=True,
+                    stop=True,
+                )
+            nc.scalar.copy(dst, p_ps[:].rearrange("p (i j) -> p i j", i=len(planes)))
+
+        for c in range(NCH):
+            level(c)
+        REST = J - CH
+        p_first = [sb(f"p_first{u}", T, F32) for u in range(2)]
+        p_rest = sb("p_rest", PACK * REST, F32)
+        rest_view = p_rest[:].rearrange("p (t j) -> p t j", t=PACK)
+        first = hidden_codes(0, 1)
+        second_layer(first, (0, 1), "z0", p_first[0][:, 0 : 2 * CH].rearrange("p (i j) -> p i j", i=2))
+        second = hidden_codes(1, 2)
+        second_layer(second, (0, 1, 2, 3), "z1", rest_view[:, :, 0:CH])
+        third = hidden_codes(2, 4)
+        second_layer(first, (2, 3), "et3", p_first[1][:, 0 : 2 * CH].rearrange("p (i j) -> p i j", i=2))
+        second_layer(third, (0, 1), "z2", rest_view[:, 0:2, CH:])
+        second_layer(third, (2, 3), "z3", rest_view[:, 2:4, CH:])
+
+        for t in range(PACK):
+            nc.vector.tensor_copy(
+                win[t][:].indirect(offsets[:, 0:OC]), p_first[t // 2][:, (t % 2) * CH : (t % 2 + 1) * CH]
+            )
+        scaled = []
+        for t, host in enumerate(("hid2", "p_first0", "p_first1")):
+            res_scaled = sb(host, T, F32)
+            nc.scalar.activation(res_scaled[:], res_sb[t][:], ACT.Copy, scale=RES_GAIN)
+            scaled.append(res_scaled)
 
         y_sb = [sb(f"y{h}", 2 * T, F32) for h in range(2)]
         y_bf = sb("y_bf", PACK * T, BF16)
@@ -252,16 +282,11 @@ def tile_moe_expert_hidden_rows_levelled_pl_kernel(
                 y_sb[h][:].rearrange("p (e c) -> p c e", e=2)[:, c0:c1, :],
             )
 
-        HO = HJ // 16
-        for t in range(2):
-            nc.vector.tensor_copy(win[t][:].indirect(offsets[:, 0:HO]), p_sb[0][0][:, t * HJ : (t + 1) * HJ])
         for t in range(PACK):
-            if t < 2:
-                nc.vector.tensor_copy(win[t][:].indirect(offsets[:, HO:]), p_sb[1][0][:, t * HJ : (t + 1) * HJ])
-            else:
-                nc.vector.tensor_copy(win[t][:].indirect(offsets[:]), p_late[:, (t - 2) * J : (t - 1) * J])
+            nc.vector.tensor_copy(win[t][:].indirect(offsets[:, OC:]), p_rest[:, t * REST : (t + 1) * REST])
             if t < PACK - 1:
-                add(t, 0, T)
+                lo = (t % 2) * T
+                nc.gpsimd.tensor_tensor(y_sb[t // 2][:, lo : lo + T], scaled[t][:], win[t][:], ALU.add)
                 store(t, 0, T)
             if t == 1:
                 nc.scalar.copy(*pair_views(0, 0, T))

@@ -146,7 +146,7 @@ def tile_moe_expert_hidden_rows_levelled_pl_kernel(
         )
 
         for t in range(PACK):
-            if t in (0, PACK - 1):
+            if t == 0:
                 x_bf = sb(f"x_bf{t}", T, BF16)
                 nc.scalar.activation(x_bf[:], x_sb[t][:], ACT.Copy)
                 nc.scalar.activation(gath_plane(0, t), x_bf[:].indirect(offsets[:]), ACT.Copy)
@@ -167,9 +167,13 @@ def tile_moe_expert_hidden_rows_levelled_pl_kernel(
         def gather_rest(t, c0, c1):
             nc.vector.tensor_copy(gath_plane(1, t)[:, c0:c1, :], x_sb[PACK + t][:].indirect(offsets[:, c0 * OC : c1 * OC]))
 
-        for t in range(PACK - 1):
+        for t in range(PACK - 2):
             gather_first(t)
             gather_rest(t, 1, NCH)
+        gather_first(PACK - 2)
+        x_late = sb("x_late", T, BF16)
+        nc.scalar.activation(x_late[:], x_sb[2 * PACK - 2][:], ACT.Copy)
+        nc.scalar.activation(gath_plane(1, PACK - 2)[:, 1:, :], x_late[:].indirect(offsets[:, OC:]), ACT.Copy)
         gather_first(PACK - 1)
         gather_rest(PACK - 1, 1, 2)
         quant_x(1, 0, 1)
@@ -192,14 +196,11 @@ def tile_moe_expert_hidden_rows_levelled_pl_kernel(
             nc.vector.bn_stats(stats[:], z_ps[c][:])
             nc.vector.bn_aggr(mv[:], stats[:])
             nc.scalar.activation(rstd[:], mv[:, 1:2], ACT.Abs_reciprocal_sqrt, bias=EPS)
-            if c == 0:
-                nc.vector.tensor_scalar(e_view, z_view, mv[:, 0:1], rstd[:], ALU.subtract, ALU.mult)
-            else:
-                negmean = sb(f"negmean{c}", 1, F32)
-                shift = sb(f"shift{c}", 1, F32)
-                nc.scalar.activation(negmean[:], mv[:, 0:1], ACT.Copy, scale=-1.0)
-                nc.scalar.activation(shift[:], negmean[:], ACT.Copy, scale=rstd[:])
-                nc.scalar.activation(e_view, z_view, ACT.Identity, bias=shift[:], scale=rstd[:])
+            negmean = sb(f"negmean{c}", 1, F32)
+            shift = sb(f"shift{c}", 1, F32)
+            nc.scalar.activation(negmean[:], mv[:, 0:1], ACT.Copy, scale=-1.0)
+            nc.scalar.activation(shift[:], negmean[:], ACT.Copy, scale=rstd[:])
+            nc.scalar.activation(e_view, z_view, ACT.Identity, bias=shift[:], scale=rstd[:])
             for t in range(PACK):
                 nc.tensor.transpose(et_ps[c][:, t * CH : (t + 1) * CH], e_sb[:, t * P : (t + 1) * P], ident[:])
 
@@ -219,7 +220,7 @@ def tile_moe_expert_hidden_rows_levelled_pl_kernel(
             nc.vector.quantize_mx(out=h_codes[:].bitcast(FP8X4), scales=h_plane[:], in_=hid[:])
             return h_codes, h_plane
 
-        def second_layer(operand, planes, bank, dst):
+        def second_layer(operand, planes, bank):
             h_codes, h_plane = operand
             width = h_plane.shape[1]
             p_ps = psum.tile([P, len(planes) * width], F32, name=bank)
@@ -233,29 +234,32 @@ def tile_moe_expert_hidden_rows_levelled_pl_kernel(
                     start=True,
                     stop=True,
                 )
-            nc.scalar.copy(dst, p_ps[:].rearrange("p (i j) -> p i j", i=len(planes)))
+            return p_ps[:].rearrange("p (i j) -> p i j", i=len(planes))
 
         for c in range(NCH):
             level(c)
-        REST = J - CH
         p_first = [sb(f"p_first{u}", T, F32) for u in range(2)]
-        p_rest = sb("p_rest", PACK * REST, F32)
-        rest_view = p_rest[:].rearrange("p (t j) -> p t j", t=PACK)
+        p_sb = sb("p_sb", PACK * J, F32)
+        p_view = p_sb[:].rearrange("p (t j) -> p t j", t=PACK)
         first = hidden_codes(0, 1)
-        second_layer(first, (0, 1), "z0", p_first[0][:, 0 : 2 * CH].rearrange("p (i j) -> p i j", i=2))
+        sums = second_layer(first, (0, 3), "z0")
+        nc.scalar.copy(p_first[0][:, 0:CH], sums[:, 0, :])
+        nc.scalar.copy(p_view[:, 3, 0:CH], sums[:, 1, :])
         second = hidden_codes(1, 2)
-        second_layer(second, (0, 1, 2, 3), "z1", rest_view[:, :, 0:CH])
+        nc.scalar.copy(p_view[:, :, CH : 2 * CH], second_layer(second, (0, 1, 2, 3), "z1"))
         third = hidden_codes(2, 4)
-        second_layer(first, (2, 3), "et3", p_first[1][:, 0 : 2 * CH].rearrange("p (i j) -> p i j", i=2))
-        second_layer(third, (0, 1), "z2", rest_view[:, 0:2, CH:])
-        second_layer(third, (2, 3), "z3", rest_view[:, 2:4, CH:])
+        nc.scalar.copy(
+            p_first[1][:, 0 : 2 * CH].rearrange("p (i j) -> p i j", i=2), second_layer(first, (1, 2), "et2")
+        )
+        nc.scalar.copy(p_view[:, 0:1, 2 * CH :], second_layer(third, (0,), "z2"))
+        nc.scalar.copy(p_view[:, 1:2, 2 * CH :], second_layer(third, (1,), "z0"))
+        nc.scalar.copy(p_view[:, 2:4, 2 * CH :], second_layer(third, (2, 3), "z3"))
 
-        for t in range(PACK):
-            nc.vector.tensor_copy(
-                win[t][:].indirect(offsets[:, 0:OC]), p_first[t // 2][:, (t % 2) * CH : (t % 2 + 1) * CH]
-            )
+        nc.vector.tensor_copy(win[0][:].indirect(offsets[:, 0:OC]), p_first[0][:, 0:CH])
+        for t in (1, 2):
+            nc.vector.tensor_copy(win[t][:].indirect(offsets[:, 0:OC]), p_first[1][:, (t - 1) * CH : t * CH])
         scaled = []
-        for t, host in enumerate(("hid2", "p_first0", "p_first1")):
+        for t, host in enumerate(("h_codes2", "p_first1", "h_plane2")):
             res_scaled = sb(host, T, F32)
             nc.scalar.activation(res_scaled[:], res_sb[t][:], ACT.Copy, scale=RES_GAIN)
             scaled.append(res_scaled)
@@ -274,7 +278,8 @@ def tile_moe_expert_hidden_rows_levelled_pl_kernel(
 
         def store(t, c0, c1):
             lo = (t % 2) * T
-            nc.sync.dma_start(out_rows[t][:, c0:c1], y_sb[t // 2][:, lo + c0 : lo + c1])
+            queue = nc.sync if t == PACK - 1 else nc.scalar
+            queue.dma_start(out_rows[t][:, c0:c1], y_sb[t // 2][:, lo + c0 : lo + c1])
 
         def pair_views(h, c0, c1):
             return (
@@ -282,14 +287,20 @@ def tile_moe_expert_hidden_rows_levelled_pl_kernel(
                 y_sb[h][:].rearrange("p (e c) -> p c e", e=2)[:, c0:c1, :],
             )
 
-        for t in range(PACK):
-            nc.vector.tensor_copy(win[t][:].indirect(offsets[:, OC:]), p_rest[:, t * REST : (t + 1) * REST])
-            if t < PACK - 1:
-                lo = (t % 2) * T
-                nc.gpsimd.tensor_tensor(y_sb[t // 2][:, lo : lo + T], scaled[t][:], win[t][:], ALU.add)
-                store(t, 0, T)
-            if t == 1:
-                nc.scalar.copy(*pair_views(0, 0, T))
+        for t in range(PACK - 1):
+            nc.vector.tensor_copy(win[t][:].indirect(offsets[:, OC:]), p_view[:, t, CH:])
+            for c0 in (0, T // 2):
+                lo = (t % 2) * T + c0
+                nc.gpsimd.tensor_tensor(
+                    y_sb[t // 2][:, lo : lo + T // 2],
+                    scaled[t][:, c0 : c0 + T // 2],
+                    win[t][:, c0 : c0 + T // 2],
+                    ALU.add,
+                )
+                if t == 1:
+                    nc.scalar.copy(*pair_views(0, c0, c0 + T // 2))
+            store(t, 0, T)
+        nc.vector.tensor_copy(win[PACK - 1][:].indirect(offsets[:]), p_view[:, PACK - 1, :])
         last = PACK - 1
         for q in range(T // QT):
             add(last, q * QT, (q + 1) * QT)
@@ -300,15 +311,12 @@ def tile_moe_expert_hidden_rows_levelled_pl_kernel(
         for q in range(2, T // QT):
             nc.vector.tensor_copy(*pair_views(1, q * QT, (q + 1) * QT))
         words_out = out_1[0].rearrange("p c r -> p (c r)").bitcast(I32)
-        for h in range(2):
-            cols = slice(h * 2 * QT, (h + 1) * 2 * QT)
+        for c0, c1 in ((0, 2 * QT), (2 * QT, 3 * QT), (3 * QT, T)):
             nc.vector.quantize_mx(
-                out=y_codes[:, cols].bitcast(FP8X4),
-                scales=y_plane[:, cols],
-                in_=y_bf[:, h * 2 * QT * PACK : (h + 1) * 2 * QT * PACK],
+                out=y_codes[:, c0:c1].bitcast(FP8X4), scales=y_plane[:, c0:c1], in_=y_bf[:, c0 * PACK : c1 * PACK]
             )
-            nc.sync.dma_start(words_out[:, cols], y_codes[:, cols].bitcast(I32))
+            nc.sync.dma_start(words_out[:, c0:c1], y_codes[:, c0:c1].bitcast(I32))
         scale_out = out_2[0].bitcast(I32).rearrange("(q r) c -> r q c", r=4)
         for r in range(4):
-            queue = nc.sync if r % 2 == 0 else nc.scalar
+            queue = nc.sync if r == 0 else nc.scalar
             queue.dma_start(scale_out[r], y_plane[r:P:32, :].bitcast(I32))

@@ -111,8 +111,8 @@ def tile_moe_expert_hidden_rows_levelled_pl_kernel(
         def weave(copy, z, c0, c1):
             cols = slice(c0 * PACK * CH, c1 * PACK * CH)
             copy(
-                woven[z][:, cols].rearrange("p (c j t) -> p c j t", j=CH, t=PACK),
-                gath[z][:, cols].rearrange("p (c t j) -> p c j t", j=CH, t=PACK),
+                woven[z][:, cols].rearrange("p (c j i t) -> p c j t i", c=c1 - c0, i=4, t=PACK),
+                gath[z][:, cols].rearrange("p (c t j i) -> p c j t i", c=c1 - c0, i=4, t=PACK),
             )
 
         def quant_x(z, c0, c1):

from contextlib import ExitStack

import concourse.mybir as mybir
from concourse.masks import make_identity

K, T, J, R, N = 1024, 1024, 512, 512, 512
FLOPS = 2 * J * K * R + 2 * J * R * N

F32 = mybir.dt.float32
BF16 = mybir.dt.bfloat16
I32 = mybir.dt.int32
U32 = mybir.dt.uint32
U16 = mybir.dt.uint16
U8 = mybir.dt.uint8
FP8X4 = mybir.dt.float8_e4m3fn_x4
FP4X4 = mybir.dt.float4_e2m1fn_x4
ALU = mybir.AluOpType
ACT = mybir.ActivationFunctionType

P = 128
PACK = 4
CH = 128
NCH = J // CH
OC = CH // 16
EPS = 0.01
RES_GAIN = 0.3
QT = 256


def tile_moe_expert_hidden_rows_levelled_pl_kernel(
    tc, xt, wa_words, wa_scales, fr, wb_words, wb_scales, res, offs, out_0, out_1, out_2
):
    nc = tc.nc
    with ExitStack() as ctx:
        keep = ctx.enter_context(tc.tile_pool(name="keep", bufs=1))
        psum = ctx.enter_context(tc.psum_pool(name="psum", bufs=1))

        def sb(name, width, dtype):
            return keep.tile([P, width], dtype, name=name, align_bytes=64)

        offsets = keep.tile([P, J // 16], U16, name="offsets")
        nc.sync.dma_start(offsets[:], offs)

        wa_plane = sb("wa_plane", 2 * R, U8)
        wb_plane_raw = sb("wb_plane_raw", N, U8)
        nc.gpsimd.memset(wb_plane_raw[:].bitcast(I32), 0)
        nc.gpsimd.memset(wa_plane[:].bitcast(I32), 0)
        warm = sb("warm", 2, F32)
        nc.vector.memset(warm[:, 0:1], 1.0)
        nc.scalar.activation(warm[:, 1:2], warm[:, 0:1], ACT.Abs_reciprocal_sqrt)

        x_rows = xt.rearrange("(z p t) c -> z t p c", p=P, t=PACK)
        x_sb = [sb(f"x{i}", T, F32) for i in range(2 * PACK)]
        wa_sb = [sb(f"wa{z}", R, U32) for z in range(2)]
        wb_raw = sb("wb_raw", 2 * N, U8)
        fr_sb = sb("fr_sb", PACK, F32)
        res_sb = [sb(f"res{t}", T, F32) for t in range(PACK)]

        def load_x(i):
            nc.sync.dma_start(x_sb[i][:], x_rows[i // PACK, i % PACK])

        def load_wa(z):
            nc.sync.dma_start(wa_sb[z][:].bitcast(I32), wa_words[z].rearrange("p n t -> p (n t)").bitcast(I32))

        def load_wa_scale(r):
            nc.sync.dma_start(
                wa_plane[r:P:32, :].bitcast(I32).rearrange("q (z c) -> q z c", z=2),
                wa_scales.bitcast(I32).rearrange("z (q r) c -> r q z c", r=4)[r],
            )

        def load_wb_scale(r):
            nc.sync.dma_start(
                wb_plane_raw[r:P:32, :].bitcast(I32),
                wb_scales[0].bitcast(I32).rearrange("(q r) c -> r q c", r=4)[r],
            )

        load_x(0)
        nc.sync.dma_start(wb_raw[:].bitcast(I32), wb_words[0].bitcast(I32))
        for r in range(4):
            load_wb_scale(r)
        for i in range(1, 6):
            load_x(i)
        load_wa_scale(0)
        load_wa_scale(1)
        load_x(6)
        load_wa_scale(2)
        load_wa_scale(3)
        load_wa(0)
        load_x(7)
        load_wa(1)
        nc.sync.dma_start(fr_sb[:], fr.rearrange("(p t) o -> p (t o)", t=PACK))
        res_rows = res.rearrange("(p t) c -> t p c", t=PACK)
        for t in range(PACK):
            nc.sync.dma_start(res_sb[t][:], res_rows[t])

        ident = sb("ident", P, F32)
        make_identity(nc, ident[:])
        win = [sb(f"win{t}", T, F32) for t in range(PACK)]
        for t in range(PACK):
            (nc.vector if t < 1 else nc.gpsimd).memset(win[t][:], 0.0)

        gath = [sb(f"gath{z}", PACK * J, BF16) for z in range(2)]
        woven = [sb(f"woven{z}", PACK * J, BF16) for z in range(2)]
        x_codes = [sb(f"x_codes{z}", J, U32) for z in range(2)]
        x_plane = [sb(f"x_plane{z}", J, U8) for z in range(2)]
        z_ps = [psum.tile([P, R], F32, name=f"z{c}") for c in range(NCH)]

        def gath_plane(z, t):
            return gath[z][:].rearrange("p (c t j) -> p c t j", c=NCH, t=PACK)[:, :, t, :]

        def weave(copy, z, c0, c1):
            cols = slice(c0 * PACK * CH, c1 * PACK * CH)
            copy(
                woven[z][:, cols].rearrange("p (c j i t) -> p c j t i", c=c1 - c0, i=4, t=PACK),
                gath[z][:, cols].rearrange("p (c t j i) -> p c j t i", c=c1 - c0, i=4, t=PACK),
            )

        def quant_x(z, c0, c1):
            nc.vector.quantize_mx(
                out=x_codes[z][:, c0 * CH : c1 * CH].bitcast(FP8X4),
                scales=x_plane[z][:, c0 * CH : c1 * CH],
                in_=woven[z][:, c0 * PACK * CH : c1 * PACK * CH],
            )

        def mm1(z, c):
            cols = slice(c * CH, (c + 1) * CH)
            nc.tensor.matmul_mx(
                out=z_ps[c][:],
                lhsT=x_codes[z][:, cols].bitcast(FP8X4),
                lhsT_scale=x_plane[z][:, cols],
                rhs=wa_sb[z][:].bitcast(FP8X4),
                rhs_scale=wa_plane[:, z * R : (z + 1) * R],
                start=(z == 0),
                stop=(z == 1),
            )

        wb_sb = sb("wb_sb", 2 * N, U8)
        wb_plane = sb("wb_plane", N, U8)
        nc.vector.tensor_copy(
            wb_sb[:].bitcast(U16).rearrange("p (t m) -> p t m", t=PACK),
            wb_raw[:].bitcast(U16).rearrange("p (m t) -> p t m", t=PACK),
        )
        nc.vector.tensor_copy(
            wb_plane[:].rearrange("p (t m) -> p t m", t=PACK),
            wb_plane_raw[:].rearrange("p (m t) -> p t m", t=PACK),
        )

        for t in range(PACK):
            if t == 0:
                x_bf = sb(f"x_bf{t}", T, BF16)
                nc.scalar.activation(x_bf[:], x_sb[t][:], ACT.Copy)
                nc.scalar.activation(gath_plane(0, t), x_bf[:].indirect(offsets[:]), ACT.Copy)
            else:
                nc.vector.tensor_copy(gath_plane(0, t), x_sb[t][:].indirect(offsets[:]))
        for h in range(2):
            weave(nc.scalar.copy, 0, 2 * h, 2 * h + 2)
            quant_x(0, 2 * h, 2 * h + 2)
            mm1(0, 2 * h)
            mm1(0, 2 * h + 1)

        def gather_first(t):
            nc.vector.tensor_copy(
                woven[1][:, 0 : PACK * CH].rearrange("p (j t) -> p t j", t=PACK)[:, t, :],
                x_sb[PACK + t][:].indirect(offsets[:, 0:OC]),
            )

        def gather_rest(t, c0, c1):
            nc.vector.tensor_copy(gath_plane(1, t)[:, c0:c1, :], x_sb[PACK + t][:].indirect(offsets[:, c0 * OC : c1 * OC]))

        for t in range(PACK - 2):
            gather_first(t)
            gather_rest(t, 1, NCH)
        gather_first(PACK - 2)
        x_late = sb("x_late", T, BF16)
        nc.scalar.activation(x_late[:], x_sb[2 * PACK - 2][:], ACT.Copy)
        nc.scalar.activation(gath_plane(1, PACK - 2)[:, 1:, :], x_late[:].indirect(offsets[:, OC:]), ACT.Copy)
        gather_first(PACK - 1)
        gather_rest(PACK - 1, 1, 2)
        quant_x(1, 0, 1)
        mm1(1, 0)
        gather_rest(PACK - 1, 2, NCH)
        for c in range(1, NCH):
            weave(nc.scalar.copy, 1, c, c + 1)
            quant_x(1, c, c + 1)
            mm1(1, c)

        et_ps = [psum.tile([P, PACK * CH], F32, name=f"et{c}") for c in range(NCH)]

        def level(c):
            stats = sb(f"stats{c}", 6, F32)
            mv = sb(f"mv{c}", 2, F32)
            rstd = sb(f"rstd{c}", 1, F32)
            e_sb = sb(f"e{c}", R, F32)
            e_view = e_sb[:].rearrange("p (t m) -> p t m", t=PACK)
            z_view = z_ps[c][:].rearrange("p (m t) -> p t m", t=PACK)
            nc.vector.bn_stats(stats[:], z_ps[c][:])
            nc.vector.bn_aggr(mv[:], stats[:])
            nc.scalar.activation(rstd[:], mv[:, 1:2], ACT.Abs_reciprocal_sqrt, bias=EPS)
            negmean = sb(f"negmean{c}", 1, F32)
            shift = sb(f"shift{c}", 1, F32)
            nc.scalar.activation(negmean[:], mv[:, 0:1], ACT.Copy, scale=-1.0)
            nc.scalar.activation(shift[:], negmean[:], ACT.Copy, scale=rstd[:])
            nc.scalar.activation(e_view, z_view, ACT.Identity, bias=shift[:], scale=rstd[:])
            for t in range(PACK):
                nc.tensor.transpose(et_ps[c][:, t * CH : (t + 1) * CH], e_sb[:, t * P : (t + 1) * P], ident[:])

        def hidden_codes(c0, c1):
            width = (c1 - c0) * CH
            hid = sb(f"hid{c0}", PACK * width, BF16)
            for c in range(c0, c1):
                lo = (c - c0) * PACK * CH
                nc.vector.tensor_tensor(
                    hid[:, lo : lo + PACK * CH].rearrange("p (j t) -> p j t", t=PACK),
                    et_ps[c][:].rearrange("p (t j) -> p j t", t=PACK),
                    fr_sb[:].unsqueeze(1).to_broadcast([P, CH, PACK]),
                    ALU.mult,
                )
            h_codes = sb(f"h_codes{c0}", width, U32)
            h_plane = sb(f"h_plane{c0}", width, U8)
            nc.vector.quantize_mx(out=h_codes[:].bitcast(FP8X4), scales=h_plane[:], in_=hid[:])
            return h_codes, h_plane

        def second_layer(operand, planes, bank):
            h_codes, h_plane = operand
            width = h_plane.shape[1]
            p_ps = psum.tile([P, len(planes) * width], F32, name=bank)
            for i, t in enumerate(planes):
                nc.tensor.matmul_mx(
                    out=p_ps[:, i * width : (i + 1) * width],
                    lhsT=wb_sb[:, 2 * t * P : 2 * (t + 1) * P].bitcast(FP4X4),
                    lhsT_scale=wb_plane[:, t * P : (t + 1) * P],
                    rhs=h_codes[:].bitcast(FP8X4),
                    rhs_scale=h_plane[:],
                    start=True,
                    stop=True,
                )
            return p_ps[:].rearrange("p (i j) -> p i j", i=len(planes))

        for c in range(NCH):
            level(c)
        p_first = [sb(f"p_first{u}", T, F32) for u in range(2)]
        p_sb = sb("p_sb", PACK * J, F32)
        p_view = p_sb[:].rearrange("p (t j) -> p t j", t=PACK)
        first = hidden_codes(0, 1)
        sums = second_layer(first, (0, 3), "z0")
        nc.scalar.copy(p_first[0][:, 0:CH], sums[:, 0, :])
        nc.scalar.copy(p_view[:, 3, 0:CH], sums[:, 1, :])
        second = hidden_codes(1, 2)
        nc.scalar.copy(p_view[:, :, CH : 2 * CH], second_layer(second, (0, 1, 2, 3), "z1"))
        third = hidden_codes(2, 4)
        nc.scalar.copy(
            p_first[1][:, 0 : 2 * CH].rearrange("p (i j) -> p i j", i=2), second_layer(first, (1, 2), "et2")
        )
        nc.scalar.copy(p_view[:, 0:1, 2 * CH :], second_layer(third, (0,), "z2"))
        nc.scalar.copy(p_view[:, 1:2, 2 * CH :], second_layer(third, (1,), "z0"))
        nc.scalar.copy(p_view[:, 2:4, 2 * CH :], second_layer(third, (2, 3), "z3"))

        nc.vector.tensor_copy(win[0][:].indirect(offsets[:, 0:OC]), p_first[0][:, 0:CH])
        for t in (1, 2):
            nc.vector.tensor_copy(win[t][:].indirect(offsets[:, 0:OC]), p_first[1][:, (t - 1) * CH : t * CH])
        scaled = []
        for t, host in enumerate(("h_codes2", "p_first1", "h_plane2")):
            res_scaled = sb(host, T, F32)
            nc.scalar.activation(res_scaled[:], res_sb[t][:], ACT.Copy, scale=RES_GAIN)
            scaled.append(res_scaled)

        y_sb = [sb(f"y{h}", 2 * T, F32) for h in range(2)]
        y_bf = sb("y_bf", PACK * T, BF16)
        y_codes = sb("y_codes", T, U32)
        y_plane = sb("y_plane", T, U8)
        out_rows = out_0.rearrange("(p t) c -> t p c", t=PACK)

        def add(t, c0, c1):
            lo = (t % 2) * T
            nc.vector.scalar_tensor_tensor(
                y_sb[t // 2][:, lo + c0 : lo + c1], res_sb[t][:, c0:c1], RES_GAIN, win[t][:, c0:c1], ALU.mult, ALU.add
            )

        def store(t, c0, c1):
            lo = (t % 2) * T
            queue = nc.sync if t == PACK - 1 else nc.scalar
            queue.dma_start(out_rows[t][:, c0:c1], y_sb[t // 2][:, lo + c0 : lo + c1])

        def pair_views(h, c0, c1):
            return (
                y_bf[:, PACK * c0 : PACK * c1].rearrange("p (c h e) -> p c h e", h=2, e=2)[:, :, h, :],
                y_sb[h][:].rearrange("p (e c) -> p c e", e=2)[:, c0:c1, :],
            )

        for t in range(PACK - 1):
            nc.vector.tensor_copy(win[t][:].indirect(offsets[:, OC:]), p_view[:, t, CH:])
            for c0 in (0, T // 2):
                lo = (t % 2) * T + c0
                nc.gpsimd.tensor_tensor(
                    y_sb[t // 2][:, lo : lo + T // 2],
                    scaled[t][:, c0 : c0 + T // 2],
                    win[t][:, c0 : c0 + T // 2],
                    ALU.add,
                )
                if t == 1:
                    nc.scalar.copy(*pair_views(0, c0, c0 + T // 2))
            store(t, 0, T)
        nc.vector.tensor_copy(win[PACK - 1][:].indirect(offsets[:]), p_view[:, PACK - 1, :])
        last = PACK - 1
        for q in range(T // QT):
            add(last, q * QT, (q + 1) * QT)
            if q % 2 == 1:
                store(last, (q - 1) * QT, (q + 1) * QT)
            if q < 2:
                nc.scalar.copy(*pair_views(1, q * QT, (q + 1) * QT))
        for q in range(2, T // QT):
            nc.vector.tensor_copy(*pair_views(1, q * QT, (q + 1) * QT))
        words_out = out_1[0].rearrange("p c r -> p (c r)").bitcast(I32)
        for c0, c1 in ((0, 2 * QT), (2 * QT, 3 * QT), (3 * QT, T)):
            nc.vector.quantize_mx(
                out=y_codes[:, c0:c1].bitcast(FP8X4), scales=y_plane[:, c0:c1], in_=y_bf[:, c0 * PACK : c1 * PACK]
            )
            nc.sync.dma_start(words_out[:, c0:c1], y_codes[:, c0:c1].bitcast(I32))
        scale_out = out_2[0].bitcast(I32).rearrange("(q r) c -> r q c", r=4)
        for r in range(4):
            queue = nc.sync if r == 0 else nc.scalar
            queue.dma_start(scale_out[r], y_plane[r:P:32, :].bitcast(I32))
